import numpy as np
import ml_dtypes


def mxq(x, axis, fmt="e4m3"):
    dtype, down = {"e4m3": (ml_dtypes.float8_e4m3fn, 7), "e5m2": (ml_dtypes.float8_e5m2, 14)}[fmt]
    v = np.moveaxis(np.asarray(x, np.float32).astype(ml_dtypes.bfloat16).astype(np.float64), axis, -1)
    blocks = v.reshape(v.shape[:-1] + (-1, 32))
    amax = np.abs(blocks).max(-1, keepdims=True)
    byte = np.maximum(np.where(amax > 0, np.frexp(amax)[1] - 1 + 127, 0) - down, 1)
    scale = np.exp2(byte - 127.0)
    codes = (blocks / scale).astype(np.float32).astype(dtype).astype(np.float64)
    return np.moveaxis((codes * scale).reshape(v.shape), -1, axis)


WIDE = False


def mx_kscale(k):
    if not WIDE:
        return np.ones(k)
    levels = np.array([10, -10, 5, -5, 0])
    if k % 512:
        return np.exp2(np.random.permutation(np.resize(levels, k // 32))).repeat(32)
    a = np.empty((k // 512, 16))
    for p in range(k // 512):
        a[p, :8] = np.random.permutation(np.resize(levels, 8))
        for g in range(8):
            far = levels[np.abs(levels - a[p, g]) >= 10]
            a[p, g + 8] = far[np.random.randint(len(far))]
    return np.exp2(a.ravel()).repeat(32)


BF16 = ml_dtypes.bfloat16


def bf(x):
    return np.asarray(x, np.float32).astype(BF16)


def f64(x):
    return np.asarray(x).astype(np.float64)


T, N, R, O = 1024, 1024, 512, 512


def draw0():
    s, t = mx_kscale(N), mx_kscale(R)
    return {
        "x": bf(np.random.standard_normal((T, N)) * s),
        "a": bf(np.random.standard_normal((N, R)) / np.sqrt(N) / s[:, None]),
        "b": bf(np.random.standard_normal((N, R)) / np.sqrt(N) / s[:, None] * t),
        "h1": bf(np.random.standard_normal((N, O)) / np.sqrt(N) / s[:, None]),
        "h2": bf(np.random.standard_normal((R, O)) / np.sqrt(R) / t[:, None]),
        "h3": bf(0.5 * np.random.standard_normal((R, O)) / np.sqrt(R) / t[:, None]),
    }


def core(x, a, b, h1, h2, h3):
    xq = mxq(f64(x), 1, "e4m3")
    p = xq @ mxq(f64(a), 0, "e4m3")
    q = xq @ mxq(f64(b), 0, "e4m3")
    k2 = p * q
    k3 = p * k2
    y1 = xq @ mxq(f64(h1), 0, "e4m3")
    y2 = mxq(k2, 1, "e4m3") @ mxq(f64(h2), 0, "e4m3")
    y3 = mxq(k3, 1, "e4m3") @ mxq(f64(h3), 0, "e4m3")
    return y1 + y2 + y3


def e4m3fn_bytes(y):
    return np.clip(np.asarray(y, np.float64), -448.0, 448.0).astype(np.float32).astype(ml_dtypes.float8_e4m3fn).view(np.uint8)


def e4m3fn_values(b):
    return np.asarray(b, np.uint8).view(ml_dtypes.float8_e4m3fn).astype(np.float64)


def setup_inputs():
    d = draw0()
    x0 = np.asarray(d['x']).astype(np.float64)
    s = (np.max(np.abs(x0), axis=(0,), keepdims=True) / 448.0).astype(np.float32)
    out = {}
    for k, v in d.items():
        if k == 'x':
            out['x_bytes'] = e4m3fn_bytes(x0 / s.astype(np.float64))
            out['x_scale'] = s
        else:
            out[k] = v
    return out


def reference(x_bytes, x_scale, a, b, h1, h2, h3):
    return core(e4m3fn_values(x_bytes) * x_scale.astype(np.float64), a, b, h1, h2, h3)

@@ -1,0 +1,265 @@
+from contextlib import ExitStack
+
+import concourse.mybir as mybir
+from concourse.masks import make_identity
+
+T, N, R, O = 1024, 1024, 512, 512
+FLOPS = 2 * T * (3 * N * R + 2 * R * O)
+
+F32 = mybir.dt.float32
+BF16 = mybir.dt.bfloat16
+U32 = mybir.dt.uint32
+U8 = mybir.dt.uint8
+FP8 = mybir.dt.float8_e4m3fn
+FP8X4 = mybir.dt.float8_e4m3fn_x4
+MULT = mybir.AluOpType.mult
+ADD = mybir.AluOpType.add
+
+P = 128
+PACK = 4
+K_PASS = P * PACK
+TILES = T // P
+WIDTH = 512
+
+
+def tile_factoredcubicvolterraequalizer_kernel(tc, x_bytes, x_scale, a, b, h1, h2, h3, out):
+    nc = tc.nc
+    x_rows = x_bytes.rearrange("(p i) k -> p i k", i=TILES)
+    out_rows = out.rearrange("(p i) o -> p i o", i=TILES)
+    sources = {
+        "a0": a[0:K_PASS, :], "a1": a[K_PASS:N, :],
+        "b0": b[0:K_PASS, :], "b1": b[K_PASS:N, :],
+        "h10": h1[0:K_PASS, :], "h11": h1[K_PASS:N, :],
+        "h2": h2, "h3": h3,
+    }
+
+    with ExitStack() as ctx:
+        keep = ctx.enter_context(tc.tile_pool(name="keep", bufs=1))
+        flow = ctx.enter_context(tc.tile_pool(name="flow", bufs=4))
+        psum = ctx.enter_context(tc.psum_pool(name="psum", bufs=2))
+        ctx.enter_context(tc.manual_schedule())
+
+        identity = keep.tile([P, P], F32, name="identity")
+        make_identity(nc, identity[:])
+        k_scale = keep.tile([P, 2, PACK], F32, name="k_scale")
+
+        raw, woven, w_codes, w_scales = {}, {}, {}, {}
+        for w in sources:
+            raw[w] = keep.tile([P, PACK, WIDTH], BF16, name="raw_" + w)
+            woven[w] = keep.tile([P, WIDTH * PACK], BF16, name="woven_" + w, align_bytes=64)
+            w_codes[w] = keep.tile([P, WIDTH], U32, name="codes_" + w, align_bytes=64)
+            w_scales[w] = keep.tile([P, WIDTH], U8, name="scales_" + w, align_bytes=64)
+        fp8_rows, wide, turned, scaled, x_codes, x_scales = {}, {}, {}, {}, {}, {}
+        p_bank, q_bank, y_bank, p_copy, k2_f32, k_bf16, k_codes, k_scales, result = {}, {}, {}, {}, {}, {}, {}, {}, {}
+
+        def load_scale():
+            nc.sync.dma_start(out=k_scale[:], in_=x_scale.rearrange("o (g p t) -> p (o g) t", p=P, t=PACK))
+
+        def load_x(first, count):
+            rows = keep.tile([P, count, N], U8, name="fp8_rows_%d" % first)
+            nc.sync.dma_start(out=rows[:], in_=x_rows[:, first : first + count, :])
+            for j in range(count):
+                fp8_rows[first + j] = rows[:, j, :]
+
+        def load_w(w):
+            nc.sync.dma_start(out=raw[w][:], in_=sources[w].rearrange("(p j) c -> p j c", j=PACK))
+
+        def copy_on(engine, dst, src):
+            if engine == "S":
+                nc.scalar.copy(out=dst, in_=src)
+            elif engine == "V":
+                nc.vector.tensor_copy(out=dst, in_=src)
+            else:
+                nc.gpsimd.tensor_scalar(out=dst, in0=src, scalar1=1.0, scalar2=0.0, op0=MULT, op1=ADD)
+
+        def weave(w, engine, lo, hi):
+            if w[0] == "h":
+                dst = woven[w][:].rearrange("p (c j) -> p c j", j=PACK)[:, lo:hi]
+                src = raw[w][:].rearrange("p j c -> p c j")[:, lo:hi]
+            else:
+                dst = woven[w][:].rearrange("p (t m e j) -> p m t e j", t=PACK, e=2, j=PACK)[:, lo // 8 : hi // 8]
+                src = raw[w][:].rearrange("p j (m e t) -> p m t e j", t=PACK, e=2)[:, lo // 8 : hi // 8]
+            copy_on(engine, dst, src)
+
+        def quant_w(w):
+            nc.vector.quantize_mx(out=w_codes[w][:].bitcast(FP8X4), scales=w_scales[w][:], in_=woven[w][:])
+
+        def widen(i):
+            wide[i] = flow.tile([P, N], BF16, name="wide")
+            nc.scalar.copy(out=wide[i][:], in_=fp8_rows[i].bitcast(FP8))
+
+        def turn(i):
+            turned[i] = psum.tile([P, 2, 2, P], F32, name="turned")
+            words = wide[i][:].bitcast(F32)
+            for g in range(2):
+                for u in range(2):
+                    nc.tensor.transpose(turned[i][:, g, u, :], words[:, 256 * g + u : 256 * (g + 1) : 2], identity[:])
+
+        def scale_x(i, g):
+            if g == 0:
+                scaled[i] = flow.tile([P, 2, P * PACK], BF16, name="scaled", align_bytes=64)
+            halves = turned[i][:].rearrange("p g u r -> p (g u r)").bitcast(BF16)
+            nc.vector.tensor_tensor(
+                out=scaled[i][:, g, :].rearrange("p (r u e) -> p r u e", u=2, e=2),
+                in0=halves.rearrange("p (g u r e) -> p g r u e", g=2, u=2, e=2)[:, g],
+                in1=k_scale[:, g, :].rearrange("p (u e) -> p u e", e=2).unsqueeze(1).to_broadcast([P, P, 2, 2]),
+                op=MULT,
+            )
+
+        def quant_x(i):
+            x_codes[i] = keep.tile([P, 2 * P], U32, name="x_codes_%d" % i, align_bytes=64)
+            x_scales[i] = keep.tile([P, 2 * P], U8, name="x_scales_%d" % i, align_bytes=64)
+            nc.vector.quantize_mx(
+                out=x_codes[i][:].bitcast(FP8X4), scales=x_scales[i][:], in_=scaled[i][:].rearrange("p g c -> p (g c)")
+            )
+
+        def project(bank, w, i):
+            for t in range(PACK):
+                cols = slice(t * P, (t + 1) * P)
+                for g in range(2):
+                    toks = slice(g * P, (g + 1) * P)
+                    name = w + str(g)
+                    nc.tensor.matmul_mx(
+                        out=bank[:, t, :],
+                        lhsT=w_codes[name][:, cols].bitcast(FP8X4), lhsT_scale=w_scales[name][:, cols],
+                        rhs=x_codes[i][:, toks].bitcast(FP8X4), rhs_scale=x_scales[i][:, toks],
+                        start=(g == 0), stop=(g == 1),
+                    )
+
+        def proj_p(i):
+            p_bank[i] = psum.tile([P, PACK, P], F32, name="p_bank")
+            project(p_bank[i], "a", i)
+
+        def proj_q(i):
+            q_bank[i] = psum.tile([P, PACK, P], F32, name="q_bank")
+            project(q_bank[i], "b", i)
+
+        def copy_p(i):
+            p_copy[i] = keep.tile([P, P, PACK], F32, name="p_copy_%d" % i)
+            nc.scalar.copy(out=p_copy[i][:], in_=p_bank[i][:].rearrange("p t r -> p r t"))
+
+        def make_k2(i):
+            k2_f32[i] = flow.tile([P, P, PACK], F32, name="k2_f32")
+            k_bf16[i] = flow.tile([P, 2, P, PACK], BF16, name="k_bf16", align_bytes=64)
+            nc.vector.tensor_tensor(
+                out=k2_f32[i][:], in0=q_bank[i][:].rearrange("p t r -> p r t"), in1=p_copy[i][:], op=MULT
+            )
+
+        def round_k2(i, engine):
+            copy_on(engine, k_bf16[i][:, 0], k2_f32[i][:])
+
+        def make_k3(i, engine):
+            on = nc.vector if engine == "V" else nc.gpsimd
+            on.tensor_tensor(out=k_bf16[i][:, 1], in0=p_copy[i][:], in1=k2_f32[i][:], op=MULT)
+
+        def quant_k(i):
+            k_codes[i] = keep.tile([P, 2 * P], U32, name="k_codes_%d" % i, align_bytes=64)
+            k_scales[i] = keep.tile([P, 2 * P], U8, name="k_scales_%d" % i, align_bytes=64)
+            nc.vector.quantize_mx(
+                out=k_codes[i][:].bitcast(FP8X4), scales=k_scales[i][:],
+                in_=k_bf16[i][:].rearrange("p s r t -> p (s r t)"),
+            )
+
+        def respond(i, part):
+            if part == 0:
+                y_bank[i] = psum.tile([P, O], F32, name="y_bank")
+                codes, scales, names = x_codes[i], x_scales[i], ("h10", "h11")
+            else:
+                codes, scales, names = k_codes[i], k_scales[i], ("h2", "h3")
+            for s in range(2):
+                toks = slice(s * P, (s + 1) * P)
+                nc.tensor.matmul_mx(
+                    out=y_bank[i][:],
+                    lhsT=codes[:, toks].bitcast(FP8X4), lhsT_scale=scales[:, toks],
+                    rhs=w_codes[names[s]][:].bitcast(FP8X4), rhs_scale=w_scales[names[s]][:],
+                    start=(part == 0 and s == 0), stop=(part == 1 and s == 1),
+                )
+
+        def store(i, engine):
+            result[i] = flow.tile([P, O], F32, name="result")
+            copy_on(engine, result[i][:], y_bank[i][:])
+            nc.sync.dma_start(out=out_rows[:, i, :], in_=result[i][:])
+
+        load_x(0, 2)
+        load_scale()
+        load_w("a0")
+        load_w("a1")
+        load_w("b0")
+        load_w("b1")
+        load_x(2, 2)
+        load_w("h10")
+        load_w("h11")
+        load_x(4, 4)
+        load_w("h2")
+        load_w("h3")
+
+        AHEAD = 3
+        widen(0)
+        widen(1)
+        turn(0)
+        turn(1)
+        names = ["a0", "a1", "b0", "b1", "h10", "h11", "h2", "h3"]
+        for n, w in enumerate(names):
+            cut = 256 if n < 4 else 224
+            weave(w, "V", 0, cut)
+            weave(w, "S", cut, 512)
+            i, g = divmod(n, 2)
+            if i < AHEAD:
+                scale_x(i, g)
+            if n > 0:
+                quant_w(names[n - 1])
+            if g == 1 and i < AHEAD:
+                quant_x(i)
+            if n == 2:
+                widen(2)
+                turn(2)
+                proj_p(0)
+            if n == 3:
+                proj_p(1)
+                widen(3)
+                turn(3)
+            if n == 4:
+                proj_q(0)
+                proj_q(1)
+            if n == 5:
+                copy_p(0)
+            if n == 6:
+                widen(4)
+                copy_p(1)
+        make_k2(0)
+        quant_w(names[-1])
+        for i in range(TILES):
+            j = i + AHEAD
+            if i > 0:
+                respond(i - 1, 1)
+            if i + 2 < TILES:
+                proj_p(i + 2)
+            if j + 1 < TILES:
+                turn(j + 1)
+            if 0 < i and j <= TILES:
+                make_k2(i)
+            if j <= TILES:
+                round_k2(i, "S")
+            if i + 2 < TILES:
+                proj_q(i + 2)
+            respond(i, 0)
+            if j < TILES:
+                scale_x(j, 0)
+            elif i + 1 < TILES:
+                if i + 2 < TILES:
+                    copy_p(i + 2)
+                make_k2(i + 1)
+                round_k2(i + 1, "S")
+            make_k3(i, "V")
+            if i > 0:
+                store(i - 1, "S")
+            if j < TILES:
+                copy_p(i + 2)
+                scale_x(j, 1)
+            if j + 2 < TILES:
+                widen(j + 2)
+            quant_k(i)
+            if j < TILES:
+                quant_x(j)
+        respond(TILES - 1, 1)
+        store(TILES - 1, "S")

@@ -20,6 +20,8 @@ PACK = 4
 K_PASS = P * PACK
 TILES = T // P
 WIDTH = 512
+DUO = 2 * P
+DUOS = T // DUO
 
 
 def tile_factoredcubicvolterraequalizer_kernel(tc, x_bytes, x_scale, a, b, h1, h2, h3, out):
@@ -49,17 +51,16 @@ def tile_factoredcubicvolterraequalizer_kernel(tc, x_bytes, x_scale, a, b, h1, h
             woven[w] = keep.tile([P, WIDTH * PACK], BF16, name="woven_" + w, align_bytes=64)
             w_codes[w] = keep.tile([P, WIDTH], U32, name="codes_" + w, align_bytes=64)
             w_scales[w] = keep.tile([P, WIDTH], U8, name="scales_" + w, align_bytes=64)
+        pooled = {}
         fp8_rows, wide, turned, scaled, x_codes, x_scales = {}, {}, {}, {}, {}, {}
         p_bank, q_bank, y_bank, p_copy, k2_f32, k_bf16, k_codes, k_scales, result = {}, {}, {}, {}, {}, {}, {}, {}, {}
 
         def load_scale():
             nc.sync.dma_start(out=k_scale[:], in_=x_scale.rearrange("o (g p t) -> p (o g) t", p=P, t=PACK))
 
-        def load_x(first, count):
-            rows = keep.tile([P, count, N], U8, name="fp8_rows_%d" % first)
-            nc.sync.dma_start(out=rows[:], in_=x_rows[:, first : first + count, :])
-            for j in range(count):
-                fp8_rows[first + j] = rows[:, j, :]
+        def load_x(d):
+            fp8_rows[d] = keep.tile([P, 2, N], U8, name="fp8_rows_%d" % d)
+            nc.sync.dma_start(out=fp8_rows[d][:], in_=x_rows[:, 2 * d : 2 * d + 2, :])
 
         def load_w(w):
             nc.sync.dma_start(out=raw[w][:], in_=sources[w].rearrange("(p j) c -> p j c", j=PACK))
@@ -74,104 +75,128 @@ def tile_factoredcubicvolterraequalizer_kernel(tc, x_bytes, x_scale, a, b, h1, h
 
         def weave(w, engine, lo, hi):
             if w[0] == "h":
-                dst = woven[w][:].rearrange("p (c j) -> p c j", j=PACK)[:, lo:hi]
-                src = raw[w][:].rearrange("p j c -> p c j")[:, lo:hi]
+                dst = woven[w][:].rearrange("p (c i j) -> p c j i", i=4, j=PACK)[:, lo // 4 : hi // 4]
+                src = raw[w][:].rearrange("p j (c i) -> p c j i", i=4)[:, lo // 4 : hi // 4]
             else:
                 dst = woven[w][:].rearrange("p (t m e j) -> p m t e j", t=PACK, e=2, j=PACK)[:, lo // 8 : hi // 8]
                 src = raw[w][:].rearrange("p j (m e t) -> p m t e j", t=PACK, e=2)[:, lo // 8 : hi // 8]
             copy_on(engine, dst, src)
 
-        def quant_w(w):
-            nc.vector.quantize_mx(out=w_codes[w][:].bitcast(FP8X4), scales=w_scales[w][:], in_=woven[w][:])
+        def slices_of(w, lo, hi):
+            return raw[w][:].rearrange("p j (m t) -> p t m j", t=PACK)[:, lo // P : hi // P]
 
-        def widen(i):
-            wide[i] = flow.tile([P, N], BF16, name="wide")
-            nc.scalar.copy(out=wide[i][:], in_=fp8_rows[i].bitcast(FP8))
+        def weave_slices(w, lo, hi):
+            dst = woven[w][:].rearrange("p (t m j) -> p t m j", t=PACK, j=PACK)[:, lo // P : hi // P]
+            nc.scalar.copy(out=dst, in_=slices_of(w, lo, hi))
 
-        def turn(i):
-            turned[i] = psum.tile([P, 2, 2, P], F32, name="turned")
-            words = wide[i][:].bitcast(F32)
+        def weave_pool(w, lo, hi):
+            pooled[w] = keep.tile([P, (hi - lo) * PACK], BF16, name="pooled", tag="pooled", align_bytes=64)
+            if w[0] == "h":
+                dst = pooled[w][:].rearrange("p (c j) -> p c j", j=PACK)
+                src = raw[w][:].rearrange("p j c -> p c j")[:, lo:hi]
+            else:
+                dst = pooled[w][:].rearrange("p (t m j) -> p t m j", m=P, j=PACK)
+                src = slices_of(w, lo, hi)
+            copy_on("G", dst, src)
+
+        def quant_w(w, lo=0, hi=WIDTH, source=None):
+            values = woven[w][:, lo * PACK : hi * PACK] if source is None else source[w][:]
+            nc.vector.quantize_mx(out=w_codes[w][:, lo:hi].bitcast(FP8X4), scales=w_scales[w][:, lo:hi], in_=values)
+
+        def widen(d, s):
+            wide[d, s] = flow.tile([P, N], BF16, name="wide")
+            nc.scalar.copy(out=wide[d, s][:], in_=fp8_rows[d][:, s, :].bitcast(FP8))
+
+        def turn(d, s):
+            words = wide[d, s][:].bitcast(F32)
             for g in range(2):
+                if s == 0:
+                    turned[d, g] = psum.tile([P, 2, 2, P], F32, name="turned", tag="turned")
                 for u in range(2):
-                    nc.tensor.transpose(turned[i][:, g, u, :], words[:, 256 * g + u : 256 * (g + 1) : 2], identity[:])
+                    nc.tensor.transpose(
+                        turned[d, g][:, u, s, :], words[:, 256 * g + u : 256 * (g + 1) : 2], identity[:]
+                    )
 
-        def scale_x(i, g):
-            if g == 0:
-                scaled[i] = flow.tile([P, 2, P * PACK], BF16, name="scaled", align_bytes=64)
-            halves = turned[i][:].rearrange("p g u r -> p (g u r)").bitcast(BF16)
+        def scale_x(d, g):
+            scaled[d, g] = flow.tile([P, DUO * PACK], BF16, name="scaled", align_bytes=64)
+            halves = turned[d, g][:].rearrange("p u s r -> p (u s r)").bitcast(BF16)
             nc.vector.tensor_tensor(
-                out=scaled[i][:, g, :].rearrange("p (r u e) -> p r u e", u=2, e=2),
-                in0=halves.rearrange("p (g u r e) -> p g r u e", g=2, u=2, e=2)[:, g],
-                in1=k_scale[:, g, :].rearrange("p (u e) -> p u e", e=2).unsqueeze(1).to_broadcast([P, P, 2, 2]),
+                out=scaled[d, g][:].rearrange("p (r u e) -> p r u e", u=2, e=2),
+                in0=halves.rearrange("p (u r e) -> p r u e", u=2, e=2),
+                in1=k_scale[:, g, :].rearrange("p (u e) -> p u e", e=2).unsqueeze(1).to_broadcast([P, DUO, 2, 2]),
                 op=MULT,
             )
 
-        def quant_x(i):
-            x_codes[i] = keep.tile([P, 2 * P], U32, name="x_codes_%d" % i, align_bytes=64)
-            x_scales[i] = keep.tile([P, 2 * P], U8, name="x_scales_%d" % i, align_bytes=64)
-            nc.vector.quantize_mx(
-                out=x_codes[i][:].bitcast(FP8X4), scales=x_scales[i][:], in_=scaled[i][:].rearrange("p g c -> p (g c)")
-            )
+        def quant_x(d, g):
+            x_codes[d, g] = keep.tile([P, DUO], U32, name="x_codes_%d_%d" % (d, g), align_bytes=64)
+            x_scales[d, g] = keep.tile([P, DUO], U8, name="x_scales_%d_%d" % (d, g), align_bytes=64)
+            nc.vector.quantize_mx(out=x_codes[d, g][:].bitcast(FP8X4), scales=x_scales[d, g][:], in_=scaled[d, g][:])
 
-        def project(bank, w, i):
-            for t in range(PACK):
-                cols = slice(t * P, (t + 1) * P)
+        def project(bank, w, d, h):
+            for e in range(2):
+                cols = slice((2 * h + e) * P, (2 * h + e + 1) * P)
                 for g in range(2):
-                    toks = slice(g * P, (g + 1) * P)
                     name = w + str(g)
                     nc.tensor.matmul_mx(
-                        out=bank[:, t, :],
+                        out=bank[:, e, :],
                         lhsT=w_codes[name][:, cols].bitcast(FP8X4), lhsT_scale=w_scales[name][:, cols],
-                        rhs=x_codes[i][:, toks].bitcast(FP8X4), rhs_scale=x_scales[i][:, toks],
+                        rhs=x_codes[d, g][:].bitcast(FP8X4), rhs_scale=x_scales[d, g][:],
                         start=(g == 0), stop=(g == 1),
                     )
 
-        def proj_p(i):
-            p_bank[i] = psum.tile([P, PACK, P], F32, name="p_bank")
-            project(p_bank[i], "a", i)
+        def proj_p(d, h):
+            p_bank[d, h] = psum.tile([P, 2, DUO], F32, name="p_bank")
+            project(p_bank[d, h], "a", d, h)
 
-        def proj_q(i):
-            q_bank[i] = psum.tile([P, PACK, P], F32, name="q_bank")
-            project(q_bank[i], "b", i)
+        def proj_q(d, h):
+            q_bank[d, h] = psum.tile([P, 2, DUO], F32, name="q_bank")
+            project(q_bank[d, h], "b", d, h)
 
-        def copy_p(i):
-            p_copy[i] = keep.tile([P, P, PACK], F32, name="p_copy_%d" % i)
-            nc.scalar.copy(out=p_copy[i][:], in_=p_bank[i][:].rearrange("p t r -> p r t"))
+        def copy_p(d, h):
+            if h == 0:
+                p_copy[d] = keep.tile([P, 2, DUO, 2], F32, name="p_copy_%d" % d)
+            nc.scalar.copy(out=p_copy[d][:, h], in_=p_bank[d, h][:].rearrange("p e r -> p r e"))
 
-        def make_k2(i):
-            k2_f32[i] = flow.tile([P, P, PACK], F32, name="k2_f32")
-            k_bf16[i] = flow.tile([P, 2, P, PACK], BF16, name="k_bf16", align_bytes=64)
+        def make_k2(d, h):
+            if h == 0:
+                k2_f32[d] = flow.tile([P, 2, DUO, 2], F32, name="k2_f32", bufs=2)
             nc.vector.tensor_tensor(
-                out=k2_f32[i][:], in0=q_bank[i][:].rearrange("p t r -> p r t"), in1=p_copy[i][:], op=MULT
+                out=k2_f32[d][:, h], in0=q_bank[d, h][:].rearrange("p e r -> p r e"), in1=p_copy[d][:, h], op=MULT
             )
 
+        def tokens_of(tile, i):
+            return tile[i // 2][:].rearrange("p h r e -> p r h e")[:, (i % 2) * P : (i % 2 + 1) * P]
+
         def round_k2(i, engine):
-            copy_on(engine, k_bf16[i][:, 0], k2_f32[i][:])
+            k_bf16[i] = flow.tile([P, 2, P, 2, 2], BF16, name="k_bf16", align_bytes=64)
+            copy_on(engine, k_bf16[i][:, 0], tokens_of(k2_f32, i))
 
         def make_k3(i, engine):
             on = nc.vector if engine == "V" else nc.gpsimd
-            on.tensor_tensor(out=k_bf16[i][:, 1], in0=p_copy[i][:], in1=k2_f32[i][:], op=MULT)
+            on.tensor_tensor(out=k_bf16[i][:, 1], in0=tokens_of(p_copy, i), in1=tokens_of(k2_f32, i), op=MULT)
 
         def quant_k(i):
             k_codes[i] = keep.tile([P, 2 * P], U32, name="k_codes_%d" % i, align_bytes=64)
             k_scales[i] = keep.tile([P, 2 * P], U8, name="k_scales_%d" % i, align_bytes=64)
             nc.vector.quantize_mx(
                 out=k_codes[i][:].bitcast(FP8X4), scales=k_scales[i][:],
-                in_=k_bf16[i][:].rearrange("p s r t -> p (s r t)"),
+                in_=k_bf16[i][:].rearrange("p s r h e -> p (s r h e)"),
             )
 
         def respond(i, part):
             if part == 0:
-                y_bank[i] = psum.tile([P, O], F32, name="y_bank")
-                codes, scales, names = x_codes[i], x_scales[i], ("h10", "h11")
-            else:
-                codes, scales, names = k_codes[i], k_scales[i], ("h2", "h3")
+                y_bank[i] = psum.tile([P, O], F32, name="y_bank", tag="turned" if i // 2 == 2 else "y_bank")
             for s in range(2):
-                toks = slice(s * P, (s + 1) * P)
+                if part == 0:
+                    toks = slice((i % 2) * P, (i % 2 + 1) * P)
+                    codes, scales, name = x_codes[i // 2, s][:, toks], x_scales[i // 2, s][:, toks], "h1" + str(s)
+                else:
+                    toks = slice(s * P, (s + 1) * P)
+                    codes, scales, name = k_codes[i][:, toks], k_scales[i][:, toks], "h" + str(2 + s)
                 nc.tensor.matmul_mx(
                     out=y_bank[i][:],
-                    lhsT=codes[:, toks].bitcast(FP8X4), lhsT_scale=scales[:, toks],
-                    rhs=w_codes[names[s]][:].bitcast(FP8X4), rhs_scale=w_scales[names[s]][:],
+                    lhsT=codes.bitcast(FP8X4), lhsT_scale=scales,
+                    rhs=w_codes[name][:].bitcast(FP8X4), rhs_scale=w_scales[name][:],
                     start=(part == 0 and s == 0), stop=(part == 1 and s == 1),
                 )
 
@@ -180,86 +205,137 @@ def tile_factoredcubicvolterraequalizer_kernel(tc, x_bytes, x_scale, a, b, h1, h
             copy_on(engine, result[i][:], y_bank[i][:])
             nc.sync.dma_start(out=out_rows[:, i, :], in_=result[i][:])
 
-        load_x(0, 2)
+        load_x(0)
         load_scale()
         load_w("a0")
+        load_x(1)
         load_w("a1")
         load_w("b0")
         load_w("b1")
-        load_x(2, 2)
         load_w("h10")
+        load_x(2)
         load_w("h11")
-        load_x(4, 4)
         load_w("h2")
         load_w("h3")
+        load_x(3)
 
-        AHEAD = 3
-        widen(0)
-        widen(1)
-        turn(0)
-        turn(1)
-        names = ["a0", "a1", "b0", "b1", "h10", "h11", "h2", "h3"]
-        for n, w in enumerate(names):
-            cut = 256 if n < 4 else 224
-            weave(w, "V", 0, cut)
-            weave(w, "S", cut, 512)
-            i, g = divmod(n, 2)
-            if i < AHEAD:
-                scale_x(i, g)
-            if n > 0:
-                quant_w(names[n - 1])
-            if g == 1 and i < AHEAD:
-                quant_x(i)
-            if n == 2:
-                widen(2)
-                turn(2)
-                proj_p(0)
-            if n == 3:
-                proj_p(1)
-                widen(3)
-                turn(3)
-            if n == 4:
-                proj_q(0)
-                proj_q(1)
-            if n == 5:
-                copy_p(0)
-            if n == 6:
-                widen(4)
-                copy_p(1)
-        make_k2(0)
-        quant_w(names[-1])
-        for i in range(TILES):
-            j = i + AHEAD
-            if i > 0:
-                respond(i - 1, 1)
-            if i + 2 < TILES:
-                proj_p(i + 2)
-            if j + 1 < TILES:
-                turn(j + 1)
-            if 0 < i and j <= TILES:
-                make_k2(i)
-            if j <= TILES:
-                round_k2(i, "S")
-            if i + 2 < TILES:
-                proj_q(i + 2)
-            respond(i, 0)
-            if j < TILES:
-                scale_x(j, 0)
-            elif i + 1 < TILES:
-                if i + 2 < TILES:
-                    copy_p(i + 2)
-                make_k2(i + 1)
-                round_k2(i + 1, "S")
-            make_k3(i, "V")
-            if i > 0:
-                store(i - 1, "S")
-            if j < TILES:
-                copy_p(i + 2)
-                scale_x(j, 1)
-            if j + 2 < TILES:
-                widen(j + 2)
-            quant_k(i)
-            if j < TILES:
-                quant_x(j)
-        respond(TILES - 1, 1)
-        store(TILES - 1, "S")
+        def weave_both(w, cut):
+            if cut > 0:
+                weave(w, "V", 0, cut)
+            if cut < 512:
+                weave(w, "S", cut, 512)
+
+        def turn_x(d):
+            for s in range(2):
+                widen(d, s)
+                turn(d, s)
+
+        def both(step, d):
+            step(d, 0)
+            step(d, 1)
+
+        turn_x(0)
+        weave_both("a0", 384)
+        scale_x(0, 0)
+        widen(1, 0)
+        widen(1, 1)
+        weave_both("a1", 256)
+        scale_x(0, 1)
+        turn(1, 0)
+        turn(1, 1)
+        quant_w("a0")
+        quant_x(0, 0)
+        quant_w("a1")
+        quant_x(0, 1)
+        both(proj_p, 0)
+        weave_both("b0", 192)
+        scale_x(1, 0)
+        weave_both("b1", 192)
+        scale_x(1, 1)
+        turn_x(2)
+        quant_w("b0")
+        quant_x(1, 0)
+        quant_w("b1")
+        both(proj_q, 0)
+        quant_x(1, 1)
+        weave_both("h10", 0)
+        both(copy_p, 0)
+        both(proj_p, 1)
+        scale_x(2, 0)
+        weave_both("h11", 0)
+        both(make_k2, 0)
+        both(proj_q, 1)
+        scale_x(2, 1)
+        round_k2(0, "S")
+        round_k2(1, "S")
+        quant_w("h10")
+        quant_x(2, 0)
+        make_k3(0, "V")
+        quant_x(2, 1)
+        make_k3(1, "V")
+        both(copy_p, 1)
+        both(proj_p, 2)
+        quant_w("h11")
+        respond(0, 0)
+        respond(1, 0)
+        weave_both("h2", 128)
+        quant_k(0)
+        quant_k(1)
+        turn_x(3)
+        weave_both("h3", 128)
+        both(make_k2, 1)
+        both(proj_q, 2)
+        quant_w("h2")
+        scale_x(3, 0)
+        quant_w("h3")
+        respond(0, 1)
+        respond(1, 1)
+        scale_x(3, 1)
+        round_k2(2, "S")
+        round_k2(3, "S")
+        both(copy_p, 2)
+        store(0, "S")
+        respond(2, 0)
+        store(1, "S")
+        respond(3, 0)
+        quant_x(3, 0)
+        make_k3(2, "V")
+        quant_x(3, 1)
+        both(proj_p, 3)
+        make_k3(3, "V")
+        make_k2(2, 0)
+        quant_k(2)
+        make_k2(2, 1)
+        quant_k(3)
+        both(proj_q, 3)
+        respond(2, 1)
+        respond(3, 1)
+        both(copy_p, 3)
+        respond(4, 0)
+        respond(5, 0)
+        round_k2(4, "S")
+        round_k2(5, "S")
+        make_k3(4, "V")
+        make_k3(5, "V")
+        store(2, "S")
+        store(3, "S")
+        make_k2(3, 0)
+        quant_k(4)
+        make_k2(3, 1)
+        quant_k(5)
+        respond(6, 0)
+        respond(7, 0)
+        respond(4, 1)
+        respond(5, 1)
+        round_k2(6, "S")
+        round_k2(7, "S")
+        make_k3(6, "V")
+        make_k3(7, "V")
+        store(4, "S")
+        store(5, "S")
+        quant_k(6)
+        respond(6, 1)
+        quant_k(7)
+        respond(7, 1)
+        store(6, "S")
+        store(7, "V")

@@ -86,8 +86,9 @@ def tile_factoredcubicvolterraequalizer_kernel(tc, x_bytes, x_scale, a, b, h1, h
             return raw[w][:].rearrange("p j (m t) -> p t m j", t=PACK)[:, lo // P : hi // P]
 
         def weave_slices(w, lo, hi):
-            dst = woven[w][:].rearrange("p (t m j) -> p t m j", t=PACK, j=PACK)[:, lo // P : hi // P]
-            nc.scalar.copy(out=dst, in_=slices_of(w, lo, hi))
+            dst = woven[w][:].rearrange("p (t m e j) -> p m t e j", t=PACK, e=2, j=PACK)[:, :, lo // P : hi // P]
+            src = raw[w][:].rearrange("p j (m e t) -> p m t e j", t=PACK, e=2)[:, :, lo // P : hi // P]
+            nc.scalar.copy(out=dst, in_=src)
 
         def weave_pool(w, lo, hi):
             pooled[w] = keep.tile([P, (hi - lo) * PACK], BF16, name="pooled", tag="pooled", align_bytes=64)
@@ -107,15 +108,12 @@ def tile_factoredcubicvolterraequalizer_kernel(tc, x_bytes, x_scale, a, b, h1, h
             wide[d, s] = flow.tile([P, N], BF16, name="wide")
             nc.scalar.copy(out=wide[d, s][:], in_=fp8_rows[d][:, s, :].bitcast(FP8))
 
-        def turn(d, s):
+        def turn(d, g, s):
             words = wide[d, s][:].bitcast(F32)
-            for g in range(2):
-                if s == 0:
-                    turned[d, g] = psum.tile([P, 2, 2, P], F32, name="turned", tag="turned")
-                for u in range(2):
-                    nc.tensor.transpose(
-                        turned[d, g][:, u, s, :], words[:, 256 * g + u : 256 * (g + 1) : 2], identity[:]
-                    )
+            if s == 0:
+                turned[d, g] = psum.tile([P, 2, 2, P], F32, name="turned", tag="turned")
+            for u in range(2):
+                nc.tensor.transpose(turned[d, g][:, u, s, :], words[:, 256 * g + u : 256 * (g + 1) : 2], identity[:])
 
         def scale_x(d, g):
             scaled[d, g] = flow.tile([P, DUO * PACK], BF16, name="scaled", align_bytes=64)
@@ -212,82 +210,88 @@ def tile_factoredcubicvolterraequalizer_kernel(tc, x_bytes, x_scale, a, b, h1, h
         load_w("a1")
         load_w("b0")
         load_w("b1")
-        load_w("h10")
         load_x(2)
+        load_w("h10")
         load_w("h11")
+        load_x(3)
         load_w("h2")
         load_w("h3")
-        load_x(3)
-
-        def weave_both(w, cut):
-            if cut > 0:
-                weave(w, "V", 0, cut)
-            if cut < 512:
-                weave(w, "S", cut, 512)
-
-        def turn_x(d):
-            for s in range(2):
-                widen(d, s)
-                turn(d, s)
 
         def both(step, d):
             step(d, 0)
             step(d, 1)
 
-        turn_x(0)
-        weave_both("a0", 384)
-        scale_x(0, 0)
-        widen(1, 0)
-        widen(1, 1)
-        weave_both("a1", 256)
-        scale_x(0, 1)
-        turn(1, 0)
-        turn(1, 1)
+        def turn_pass(d, g):
+            turn(d, g, 0)
+            turn(d, g, 1)
+
+        HALF = WIDTH // 2
+        both(widen, 0)
+        for s in range(2):
+            turn(0, 0, s)
+            turn(0, 1, s)
+        weave("a0", "V", 0, 384)
+        weave("a0", "S", 384, 512)
+        weave_pool("a1", HALF, WIDTH)
+        both(widen, 1)
+        for g in range(2):
+            scale_x(0, g)
+            turn_pass(1, g)
+        weave_slices("a1", 0, HALF)
         quant_w("a0")
         quant_x(0, 0)
-        quant_w("a1")
+        quant_w("a1", 0, HALF)
         quant_x(0, 1)
+        quant_w("a1", HALF, WIDTH, pooled)
         both(proj_p, 0)
-        weave_both("b0", 192)
-        scale_x(1, 0)
-        weave_both("b1", 192)
-        scale_x(1, 1)
-        turn_x(2)
+        weave("b0", "S", 0, WIDTH)
+        weave_pool("b1", HALF, WIDTH)
+        weave_slices("b1", 0, HALF)
+        both(widen, 2)
+        for g in range(2):
+            scale_x(1, g)
+            turn_pass(2, g)
         quant_w("b0")
         quant_x(1, 0)
-        quant_w("b1")
-        both(proj_q, 0)
+        quant_w("b1", 0, HALF)
         quant_x(1, 1)
-        weave_both("h10", 0)
+        quant_w("b1", HALF, WIDTH, pooled)
+        both(proj_q, 0)
         both(copy_p, 0)
         both(proj_p, 1)
+        weave_pool("h11", 0, WIDTH)
+        weave("h10", "S", 0, WIDTH)
+        both(widen, 3)
         scale_x(2, 0)
-        weave_both("h11", 0)
         both(make_k2, 0)
         both(proj_q, 1)
         scale_x(2, 1)
+        both(turn_pass, 3)
         round_k2(0, "S")
         round_k2(1, "S")
-        quant_w("h10")
-        quant_x(2, 0)
-        make_k3(0, "V")
-        quant_x(2, 1)
-        make_k3(1, "V")
         both(copy_p, 1)
+        weave("h2", "S", 0, WIDTH)
+        quant_x(2, 0)
+        quant_w("h10")
+        quant_x(2, 1)
         both(proj_p, 2)
-        quant_w("h11")
-        respond(0, 0)
-        respond(1, 0)
-        weave_both("h2", 128)
+        make_k3(0, "V")
+        make_k3(1, "V")
         quant_k(0)
         quant_k(1)
-        turn_x(3)
-        weave_both("h3", 128)
-        both(make_k2, 1)
+        quant_w("h11", 0, WIDTH, pooled)
+        respond(0, 0)
+        respond(1, 0)
+        weave_pool("h3", HALF, WIDTH)
+        weave("h3", "S", 0, HALF)
+        make_k2(1, 0)
+        scale_x(3, 0)
+        make_k2(1, 1)
         both(proj_q, 2)
         quant_w("h2")
-        scale_x(3, 0)
-        quant_w("h3")
+        quant_x(3, 0)
+        quant_w("h3", HALF, WIDTH, pooled)
+        quant_w("h3", 0, HALF)
         respond(0, 1)
         respond(1, 1)
         scale_x(3, 1)
@@ -298,7 +302,6 @@ def tile_factoredcubicvolterraequalizer_kernel(tc, x_bytes, x_scale, a, b, h1, h
         respond(2, 0)
         store(1, "S")
         respond(3, 0)
-        quant_x(3, 0)
         make_k3(2, "V")
         quant_x(3, 1)
         both(proj_p, 3)
@@ -323,10 +326,10 @@ def tile_factoredcubicvolterraequalizer_kernel(tc, x_bytes, x_scale, a, b, h1, h
         quant_k(4)
         make_k2(3, 1)
         quant_k(5)
-        respond(6, 0)
-        respond(7, 0)
         respond(4, 1)
+        respond(6, 0)
         respond(5, 1)
+        respond(7, 0)
         round_k2(6, "S")
         round_k2(7, "S")
         make_k3(6, "V")

@@ -104,9 +104,9 @@ def tile_factoredcubicvolterraequalizer_kernel(tc, x_bytes, x_scale, a, b, h1, h
             values = woven[w][:, lo * PACK : hi * PACK] if source is None else source[w][:]
             nc.vector.quantize_mx(out=w_codes[w][:, lo:hi].bitcast(FP8X4), scales=w_scales[w][:, lo:hi], in_=values)
 
-        def widen(d, s):
+        def widen(d, s, engine="S"):
             wide[d, s] = flow.tile([P, N], BF16, name="wide")
-            nc.scalar.copy(out=wide[d, s][:], in_=fp8_rows[d][:, s, :].bitcast(FP8))
+            copy_on(engine, wide[d, s][:], fp8_rows[d][:, s, :].bitcast(FP8))
 
         def turn(d, g, s):
             words = wide[d, s][:].bitcast(F32)
@@ -173,29 +173,32 @@ def tile_factoredcubicvolterraequalizer_kernel(tc, x_bytes, x_scale, a, b, h1, h
             on = nc.vector if engine == "V" else nc.gpsimd
             on.tensor_tensor(out=k_bf16[i][:, 1], in0=tokens_of(p_copy, i), in1=tokens_of(k2_f32, i), op=MULT)
 
-        def quant_k(i):
-            k_codes[i] = keep.tile([P, 2 * P], U32, name="k_codes_%d" % i, align_bytes=64)
-            k_scales[i] = keep.tile([P, 2 * P], U8, name="k_scales_%d" % i, align_bytes=64)
+        def quant_k(i, first=0, last=1):
+            if first == 0:
+                k_codes[i] = keep.tile([P, 2 * P], U32, name="k_codes_%d" % i, align_bytes=64)
+                k_scales[i] = keep.tile([P, 2 * P], U8, name="k_scales_%d" % i, align_bytes=64)
+            cols = slice(first * P, (last + 1) * P)
             nc.vector.quantize_mx(
-                out=k_codes[i][:].bitcast(FP8X4), scales=k_scales[i][:],
-                in_=k_bf16[i][:].rearrange("p s r h e -> p (s r h e)"),
+                out=k_codes[i][:, cols].bitcast(FP8X4), scales=k_scales[i][:, cols],
+                in_=k_bf16[i][:, first : last + 1].rearrange("p s r h e -> p (s r h e)"),
             )
 
-        def respond(i, part):
-            if part == 0:
-                y_bank[i] = psum.tile([P, O], F32, name="y_bank", tag="turned" if i // 2 == 2 else "y_bank")
-            for s in range(2):
-                if part == 0:
+        def respond(i, names):
+            for name in names:
+                if name == "h10":
+                    y_bank[i] = psum.tile([P, O], F32, name="y_bank", tag="turned" if (i // 2) % 2 else "y_bank")
+                if name in ("h10", "h11"):
                     toks = slice((i % 2) * P, (i % 2 + 1) * P)
-                    codes, scales, name = x_codes[i // 2, s][:, toks], x_scales[i // 2, s][:, toks], "h1" + str(s)
+                    g = int(name[2])
+                    codes, scales = x_codes[i // 2, g][:, toks], x_scales[i // 2, g][:, toks]
                 else:
-                    toks = slice(s * P, (s + 1) * P)
-                    codes, scales, name = k_codes[i][:, toks], k_scales[i][:, toks], "h" + str(2 + s)
+                    toks = slice(0, P) if name == "h2" else slice(P, 2 * P)
+                    codes, scales = k_codes[i][:, toks], k_scales[i][:, toks]
                 nc.tensor.matmul_mx(
                     out=y_bank[i][:],
                     lhsT=codes.bitcast(FP8X4), lhsT_scale=scales,
                     rhs=w_codes[name][:].bitcast(FP8X4), rhs_scale=w_scales[name][:],
-                    start=(part == 0 and s == 0), stop=(part == 1 and s == 1),
+                    start=(name == "h10"), stop=(name == "h3"),
                 )
 
         def store(i, engine):
@@ -206,8 +209,8 @@ def tile_factoredcubicvolterraequalizer_kernel(tc, x_bytes, x_scale, a, b, h1, h
         load_x(0)
         load_scale()
         load_w("a0")
-        load_x(1)
         load_w("a1")
+        load_x(1)
         load_w("b0")
         load_w("b1")
         load_x(2)
@@ -226,25 +229,26 @@ def tile_factoredcubicvolterraequalizer_kernel(tc, x_bytes, x_scale, a, b, h1, h
             turn(d, g, 1)
 
         HALF = WIDTH // 2
-        both(widen, 0)
-        for s in range(2):
-            turn(0, 0, s)
-            turn(0, 1, s)
+        LINEAR, FEATURES = ("h10", "h11"), ("h2", "h3")
+        widen(0, 0, "V")
+        widen(0, 1)
+        both(turn_pass, 0)
         weave("a0", "V", 0, 384)
-        weave("a0", "S", 384, 512)
+        weave("a0", "S", 384, WIDTH)
         weave_pool("a1", HALF, WIDTH)
+        weave_slices("a1", 0, HALF)
         both(widen, 1)
         for g in range(2):
             scale_x(0, g)
             turn_pass(1, g)
-        weave_slices("a1", 0, HALF)
         quant_w("a0")
         quant_x(0, 0)
+        weave("b0", "V", 0, 256)
         quant_w("a1", 0, HALF)
         quant_x(0, 1)
         quant_w("a1", HALF, WIDTH, pooled)
         both(proj_p, 0)
-        weave("b0", "S", 0, WIDTH)
+        weave("b0", "S", 256, WIDTH)
         weave_pool("b1", HALF, WIDTH)
         weave_slices("b1", 0, HALF)
         both(widen, 2)
@@ -280,42 +284,44 @@ def tile_factoredcubicvolterraequalizer_kernel(tc, x_bytes, x_scale, a, b, h1, h
         quant_k(0)
         quant_k(1)
         quant_w("h11", 0, WIDTH, pooled)
-        respond(0, 0)
-        respond(1, 0)
+        respond(0, LINEAR)
+        respond(1, LINEAR)
         weave_pool("h3", HALF, WIDTH)
         weave("h3", "S", 0, HALF)
         make_k2(1, 0)
         scale_x(3, 0)
         make_k2(1, 1)
         both(proj_q, 2)
+        scale_x(3, 1)
+        respond(2, LINEAR)
         quant_w("h2")
+        respond(0, ["h2"])
+        respond(1, ["h2"])
+        respond(3, LINEAR)
         quant_x(3, 0)
         quant_w("h3", HALF, WIDTH, pooled)
         quant_w("h3", 0, HALF)
-        respond(0, 1)
-        respond(1, 1)
-        scale_x(3, 1)
+        quant_x(3, 1)
+        respond(0, ["h3"])
+        respond(1, ["h3"])
+        both(copy_p, 2)
         round_k2(2, "S")
         round_k2(3, "S")
-        both(copy_p, 2)
-        store(0, "S")
-        respond(2, 0)
-        store(1, "S")
-        respond(3, 0)
-        make_k3(2, "V")
-        quant_x(3, 1)
         both(proj_p, 3)
+        store(0, "S")
+        store(1, "S")
+        make_k3(2, "V")
         make_k3(3, "V")
         make_k2(2, 0)
         quant_k(2)
         make_k2(2, 1)
         quant_k(3)
+        respond(4, LINEAR)
         both(proj_q, 3)
-        respond(2, 1)
-        respond(3, 1)
+        respond(2, FEATURES)
+        respond(3, FEATURES)
+        respond(5, LINEAR)
         both(copy_p, 3)
-        respond(4, 0)
-        respond(5, 0)
         round_k2(4, "S")
         round_k2(5, "S")
         make_k3(4, "V")
@@ -325,20 +331,22 @@ def tile_factoredcubicvolterraequalizer_kernel(tc, x_bytes, x_scale, a, b, h1, h
         make_k2(3, 0)
         quant_k(4)
         make_k2(3, 1)
-        quant_k(5)
-        respond(4, 1)
-        respond(6, 0)
-        respond(5, 1)
-        respond(7, 0)
+        respond(6, LINEAR)
+        respond(4, FEATURES)
+        respond(7, LINEAR)
         round_k2(6, "S")
         round_k2(7, "S")
         make_k3(6, "V")
+        quant_k(5)
+        respond(5, FEATURES)
+        quant_k(6)
+        respond(6, FEATURES)
         make_k3(7, "V")
         store(4, "S")
         store(5, "S")
-        quant_k(6)
-        respond(6, 1)
-        quant_k(7)
-        respond(7, 1)
         store(6, "S")
+        quant_k(7, 0, 0)
+        respond(7, ["h2"])
+        quant_k(7, 1, 1)
+        respond(7, ["h3"])
         store(7, "V")

from contextlib import ExitStack

import concourse.mybir as mybir
from concourse.masks import make_identity

T, N, R, O = 1024, 1024, 512, 512
FLOPS = 2 * T * (3 * N * R + 2 * R * O)

F32 = mybir.dt.float32
BF16 = mybir.dt.bfloat16
U32 = mybir.dt.uint32
U8 = mybir.dt.uint8
FP8 = mybir.dt.float8_e4m3fn
FP8X4 = mybir.dt.float8_e4m3fn_x4
MULT = mybir.AluOpType.mult
ADD = mybir.AluOpType.add

P = 128
PACK = 4
K_PASS = P * PACK
TILES = T // P
WIDTH = 512
DUO = 2 * P
DUOS = T // DUO


def tile_factoredcubicvolterraequalizer_kernel(tc, x_bytes, x_scale, a, b, h1, h2, h3, out):
    nc = tc.nc
    x_rows = x_bytes.rearrange("(p i) k -> p i k", i=TILES)
    out_rows = out.rearrange("(p i) o -> p i o", i=TILES)
    sources = {
        "a0": a[0:K_PASS, :], "a1": a[K_PASS:N, :],
        "b0": b[0:K_PASS, :], "b1": b[K_PASS:N, :],
        "h10": h1[0:K_PASS, :], "h11": h1[K_PASS:N, :],
        "h2": h2, "h3": h3,
    }

    with ExitStack() as ctx:
        keep = ctx.enter_context(tc.tile_pool(name="keep", bufs=1))
        flow = ctx.enter_context(tc.tile_pool(name="flow", bufs=4))
        psum = ctx.enter_context(tc.psum_pool(name="psum", bufs=2))
        ctx.enter_context(tc.manual_schedule())

        identity = keep.tile([P, P], F32, name="identity")
        make_identity(nc, identity[:])
        k_scale = keep.tile([P, 2, PACK], F32, name="k_scale")

        raw, woven, w_codes, w_scales = {}, {}, {}, {}
        for w in sources:
            raw[w] = keep.tile([P, PACK, WIDTH], BF16, name="raw_" + w)
            woven[w] = keep.tile([P, WIDTH * PACK], BF16, name="woven_" + w, align_bytes=64)
            w_codes[w] = keep.tile([P, WIDTH], U32, name="codes_" + w, align_bytes=64)
            w_scales[w] = keep.tile([P, WIDTH], U8, name="scales_" + w, align_bytes=64)
        pooled = {}
        fp8_rows, wide, turned, scaled, x_codes, x_scales = {}, {}, {}, {}, {}, {}
        p_bank, q_bank, y_bank, p_copy, k2_f32, k_bf16, k_codes, k_scales, result = {}, {}, {}, {}, {}, {}, {}, {}, {}

        def load_scale():
            nc.sync.dma_start(out=k_scale[:], in_=x_scale.rearrange("o (g p t) -> p (o g) t", p=P, t=PACK))

        def load_x(d):
            fp8_rows[d] = keep.tile([P, 2, N], U8, name="fp8_rows_%d" % d)
            nc.sync.dma_start(out=fp8_rows[d][:], in_=x_rows[:, 2 * d : 2 * d + 2, :])

        def load_w(w):
            nc.sync.dma_start(out=raw[w][:], in_=sources[w].rearrange("(p j) c -> p j c", j=PACK))

        def copy_on(engine, dst, src):
            if engine == "S":
                nc.scalar.copy(out=dst, in_=src)
            elif engine == "V":
                nc.vector.tensor_copy(out=dst, in_=src)
            else:
                nc.gpsimd.tensor_scalar(out=dst, in0=src, scalar1=1.0, scalar2=0.0, op0=MULT, op1=ADD)

        def weave(w, engine, lo, hi):
            if w[0] == "h":
                dst = woven[w][:].rearrange("p (c i j) -> p c j i", i=4, j=PACK)[:, lo // 4 : hi // 4]
                src = raw[w][:].rearrange("p j (c i) -> p c j i", i=4)[:, lo // 4 : hi // 4]
            else:
                dst = woven[w][:].rearrange("p (t m e j) -> p m t e j", t=PACK, e=2, j=PACK)[:, lo // 8 : hi // 8]
                src = raw[w][:].rearrange("p j (m e t) -> p m t e j", t=PACK, e=2)[:, lo // 8 : hi // 8]
            copy_on(engine, dst, src)

        def slices_of(w, lo, hi):
            return raw[w][:].rearrange("p j (m t) -> p t m j", t=PACK)[:, lo // P : hi // P]

        def weave_slices(w, lo, hi):
            dst = woven[w][:].rearrange("p (t m e j) -> p m t e j", t=PACK, e=2, j=PACK)[:, :, lo // P : hi // P]
            src = raw[w][:].rearrange("p j (m e t) -> p m t e j", t=PACK, e=2)[:, :, lo // P : hi // P]
            nc.scalar.copy(out=dst, in_=src)

        def weave_pool(w, lo, hi):
            pooled[w] = keep.tile([P, (hi - lo) * PACK], BF16, name="pooled", tag="pooled", align_bytes=64)
            if w[0] == "h":
                dst = pooled[w][:].rearrange("p (c j) -> p c j", j=PACK)
                src = raw[w][:].rearrange("p j c -> p c j")[:, lo:hi]
            else:
                dst = pooled[w][:].rearrange("p (t m j) -> p t m j", m=P, j=PACK)
                src = slices_of(w, lo, hi)
            copy_on("G", dst, src)

        def quant_w(w, lo=0, hi=WIDTH, source=None):
            values = woven[w][:, lo * PACK : hi * PACK] if source is None else source[w][:]
            nc.vector.quantize_mx(out=w_codes[w][:, lo:hi].bitcast(FP8X4), scales=w_scales[w][:, lo:hi], in_=values)

        def widen(d, s, engine="S"):
            wide[d, s] = flow.tile([P, N], BF16, name="wide")
            copy_on(engine, wide[d, s][:], fp8_rows[d][:, s, :].bitcast(FP8))

        def turn(d, g, s):
            words = wide[d, s][:].bitcast(F32)
            if s == 0:
                turned[d, g] = psum.tile([P, 2, 2, P], F32, name="turned", tag="turned")
            for u in range(2):
                nc.tensor.transpose(turned[d, g][:, u, s, :], words[:, 256 * g + u : 256 * (g + 1) : 2], identity[:])

        def scale_x(d, g):
            scaled[d, g] = flow.tile([P, DUO * PACK], BF16, name="scaled", align_bytes=64)
            halves = turned[d, g][:].rearrange("p u s r -> p (u s r)").bitcast(BF16)
            nc.vector.tensor_tensor(
                out=scaled[d, g][:].rearrange("p (r u e) -> p r u e", u=2, e=2),
                in0=halves.rearrange("p (u r e) -> p r u e", u=2, e=2),
                in1=k_scale[:, g, :].rearrange("p (u e) -> p u e", e=2).unsqueeze(1).to_broadcast([P, DUO, 2, 2]),
                op=MULT,
            )

        def quant_x(d, g):
            x_codes[d, g] = keep.tile([P, DUO], U32, name="x_codes_%d_%d" % (d, g), align_bytes=64)
            x_scales[d, g] = keep.tile([P, DUO], U8, name="x_scales_%d_%d" % (d, g), align_bytes=64)
            nc.vector.quantize_mx(out=x_codes[d, g][:].bitcast(FP8X4), scales=x_scales[d, g][:], in_=scaled[d, g][:])

        def project(bank, w, d, h):
            for e in range(2):
                cols = slice((2 * h + e) * P, (2 * h + e + 1) * P)
                for g in range(2):
                    name = w + str(g)
                    nc.tensor.matmul_mx(
                        out=bank[:, e, :],
                        lhsT=w_codes[name][:, cols].bitcast(FP8X4), lhsT_scale=w_scales[name][:, cols],
                        rhs=x_codes[d, g][:].bitcast(FP8X4), rhs_scale=x_scales[d, g][:],
                        start=(g == 0), stop=(g == 1),
                    )

        def proj_p(d, h):
            p_bank[d, h] = psum.tile([P, 2, DUO], F32, name="p_bank")
            project(p_bank[d, h], "a", d, h)

        def proj_q(d, h):
            q_bank[d, h] = psum.tile([P, 2, DUO], F32, name="q_bank")
            project(q_bank[d, h], "b", d, h)

        def copy_p(d, h):
            if h == 0:
                p_copy[d] = keep.tile([P, 2, DUO, 2], F32, name="p_copy_%d" % d)
            nc.scalar.copy(out=p_copy[d][:, h], in_=p_bank[d, h][:].rearrange("p e r -> p r e"))

        def make_k2(d, h):
            if h == 0:
                k2_f32[d] = flow.tile([P, 2, DUO, 2], F32, name="k2_f32", bufs=2)
            nc.vector.tensor_tensor(
                out=k2_f32[d][:, h], in0=q_bank[d, h][:].rearrange("p e r -> p r e"), in1=p_copy[d][:, h], op=MULT
            )

        def tokens_of(tile, i):
            return tile[i // 2][:].rearrange("p h r e -> p r h e")[:, (i % 2) * P : (i % 2 + 1) * P]

        def round_k2(i, engine):
            k_bf16[i] = flow.tile([P, 2, P, 2, 2], BF16, name="k_bf16", align_bytes=64)
            copy_on(engine, k_bf16[i][:, 0], tokens_of(k2_f32, i))

        def make_k3(i, engine):
            on = nc.vector if engine == "V" else nc.gpsimd
            on.tensor_tensor(out=k_bf16[i][:, 1], in0=tokens_of(p_copy, i), in1=tokens_of(k2_f32, i), op=MULT)

        def quant_k(i, first=0, last=1):
            if first == 0:
                k_codes[i] = keep.tile([P, 2 * P], U32, name="k_codes_%d" % i, align_bytes=64)
                k_scales[i] = keep.tile([P, 2 * P], U8, name="k_scales_%d" % i, align_bytes=64)
            cols = slice(first * P, (last + 1) * P)
            nc.vector.quantize_mx(
                out=k_codes[i][:, cols].bitcast(FP8X4), scales=k_scales[i][:, cols],
                in_=k_bf16[i][:, first : last + 1].rearrange("p s r h e -> p (s r h e)"),
            )

        def respond(i, names):
            for name in names:
                if name == "h10":
                    y_bank[i] = psum.tile([P, O], F32, name="y_bank", tag="turned" if (i // 2) % 2 else "y_bank")
                if name in ("h10", "h11"):
                    toks = slice((i % 2) * P, (i % 2 + 1) * P)
                    g = int(name[2])
                    codes, scales = x_codes[i // 2, g][:, toks], x_scales[i // 2, g][:, toks]
                else:
                    toks = slice(0, P) if name == "h2" else slice(P, 2 * P)
                    codes, scales = k_codes[i][:, toks], k_scales[i][:, toks]
                nc.tensor.matmul_mx(
                    out=y_bank[i][:],
                    lhsT=codes.bitcast(FP8X4), lhsT_scale=scales,
                    rhs=w_codes[name][:].bitcast(FP8X4), rhs_scale=w_scales[name][:],
                    start=(name == "h10"), stop=(name == "h3"),
                )

        def store(i, engine):
            result[i] = flow.tile([P, O], F32, name="result")
            copy_on(engine, result[i][:], y_bank[i][:])
            nc.sync.dma_start(out=out_rows[:, i, :], in_=result[i][:])

        load_x(0)
        load_scale()
        load_w("a0")
        load_w("a1")
        load_x(1)
        load_w("b0")
        load_w("b1")
        load_x(2)
        load_w("h10")
        load_w("h11")
        load_x(3)
        load_w("h2")
        load_w("h3")

        def both(step, d):
            step(d, 0)
            step(d, 1)

        def turn_pass(d, g):
            turn(d, g, 0)
            turn(d, g, 1)

        HALF = WIDTH // 2
        LINEAR, FEATURES = ("h10", "h11"), ("h2", "h3")
        widen(0, 0, "V")
        widen(0, 1)
        both(turn_pass, 0)
        weave("a0", "V", 0, 384)
        weave("a0", "S", 384, WIDTH)
        weave_pool("a1", HALF, WIDTH)
        weave_slices("a1", 0, HALF)
        both(widen, 1)
        for g in range(2):
            scale_x(0, g)
            turn_pass(1, g)
        quant_w("a0")
        quant_x(0, 0)
        weave("b0", "V", 0, 256)
        quant_w("a1", 0, HALF)
        quant_x(0, 1)
        quant_w("a1", HALF, WIDTH, pooled)
        both(proj_p, 0)
        weave("b0", "S", 256, WIDTH)
        weave_pool("b1", HALF, WIDTH)
        weave_slices("b1", 0, HALF)
        both(widen, 2)
        for g in range(2):
            scale_x(1, g)
            turn_pass(2, g)
        quant_w("b0")
        quant_x(1, 0)
        quant_w("b1", 0, HALF)
        quant_x(1, 1)
        quant_w("b1", HALF, WIDTH, pooled)
        both(proj_q, 0)
        both(copy_p, 0)
        both(proj_p, 1)
        weave_pool("h11", 0, WIDTH)
        weave("h10", "S", 0, WIDTH)
        both(widen, 3)
        scale_x(2, 0)
        both(make_k2, 0)
        both(proj_q, 1)
        scale_x(2, 1)
        both(turn_pass, 3)
        round_k2(0, "S")
        round_k2(1, "S")
        both(copy_p, 1)
        weave("h2", "S", 0, WIDTH)
        quant_x(2, 0)
        quant_w("h10")
        quant_x(2, 1)
        both(proj_p, 2)
        make_k3(0, "V")
        make_k3(1, "V")
        quant_k(0)
        quant_k(1)
        quant_w("h11", 0, WIDTH, pooled)
        respond(0, LINEAR)
        respond(1, LINEAR)
        weave_pool("h3", HALF, WIDTH)
        weave("h3", "S", 0, HALF)
        make_k2(1, 0)
        scale_x(3, 0)
        make_k2(1, 1)
        both(proj_q, 2)
        scale_x(3, 1)
        respond(2, LINEAR)
        quant_w("h2")
        respond(0, ["h2"])
        respond(1, ["h2"])
        respond(3, LINEAR)
        quant_x(3, 0)
        quant_w("h3", HALF, WIDTH, pooled)
        quant_w("h3", 0, HALF)
        quant_x(3, 1)
        respond(0, ["h3"])
        respond(1, ["h3"])
        both(copy_p, 2)
        round_k2(2, "S")
        round_k2(3, "S")
        both(proj_p, 3)
        store(0, "S")
        store(1, "S")
        make_k3(2, "V")
        make_k3(3, "V")
        make_k2(2, 0)
        quant_k(2)
        make_k2(2, 1)
        quant_k(3)
        respond(4, LINEAR)
        both(proj_q, 3)
        respond(2, FEATURES)
        respond(3, FEATURES)
        respond(5, LINEAR)
        both(copy_p, 3)
        round_k2(4, "S")
        round_k2(5, "S")
        make_k3(4, "V")
        make_k3(5, "V")
        store(2, "S")
        store(3, "S")
        make_k2(3, 0)
        quant_k(4)
        make_k2(3, 1)
        respond(6, LINEAR)
        respond(4, FEATURES)
        respond(7, LINEAR)
        round_k2(6, "S")
        round_k2(7, "S")
        make_k3(6, "V")
        quant_k(5)
        respond(5, FEATURES)
        quant_k(6)
        respond(6, FEATURES)
        make_k3(7, "V")
        store(4, "S")
        store(5, "S")
        store(6, "S")
        quant_k(7, 0, 0)
        respond(7, ["h2"])
        quant_k(7, 1, 1)
        respond(7, ["h3"])
        store(7, "V")
